import numpy as np, ml_dtypes
CORES = [50,106,114,52,108,116]
N = 6
import mx_ref
NC = 128
BF = ml_dtypes.bfloat16
def cut(t, i, w=512):
    return t[:, w * i:w * i + w]
def tile(rs):
    return np.stack(rs, axis=2).reshape(128, -1).astype(BF)
def onehot(t, r):
    own, p, b = t[:, :NC], t[:, NC:2 * NC], t[:, 2 * NC:]
    return tile([((own == r) & (p == np.arange(128)[:, None]) & (b == f)).astype(np.float32) for f in range(4)])
def setup_inputs(rng):
    def f(*shape):
        return mx_ref.flush((rng.standard_normal(shape, dtype=np.float32) * np.exp2(rng.integers(-2, 3, shape[:-1] + (1,)))).astype(BF))
    t = np.concatenate([rng.integers(0, N, (N, 1, NC)), rng.integers(0, 128, (N, 1, NC)), rng.integers(0, 4, (N, 1, NC))], axis=2)
    return {"tg": np.broadcast_to(t, (N, 128, 3 * NC)).astype(BF).copy(), "tab": f(N, 128, 4 * 512), "w": f(N, 128, 512)}
def setup_inputs_blocks(rng):
    d = setup_inputs(rng)
    for k in ("tab", "w"): d[k] = mx_ref.spread(d[k], rng, 4)
    return d
def setup_inputs_wide(rng):
    d = setup_inputs(rng)
    for k in ("tab", "w"): d[k] = mx_ref.flush((d[k].astype(np.float32) * np.exp2(rng.integers(-6, 7, (N, 1, 1))).astype(np.float32)).astype(BF))
    return d
def setup_inputs_hot(rng):
    d = setup_inputs(rng); t = d["tg"].astype(np.float32); t[:, :, :NC] = rng.integers(0, N); t[:, :, NC:2 * NC] = np.broadcast_to(rng.integers(0, 4, (N, 1, NC)), (N, 128, NC))
    d["tg"] = t.astype(BF)
    return d
def reference(tg, tab, w):
    y = np.zeros((N, 128, NC), np.float32)
    for j in range(N):
        qw = mx_ref.quantize(w[j])
        for r in range(N):
            o = mx_ref.quantize(onehot(tg[j].astype(np.float32), r))
            e = mx_ref.quantize(tile([mx_ref.matmul(mx_ref.quantize(cut(tab[r], f)), o) for f in range(4)]))
            p = mx_ref.matmul(qw, e)
            y[j] = p if r == 0 else y[j] + p
    return {"y": y}

@@ -1,0 +1,363 @@
+from concourse.bass import DstId, RemoteDMATransfer
+from concourse.mybir import dt, AluOpType, ActivationFunctionType
+
+N = 6
+NC = 128
+MX = "float8_e4m3fn_x4"
+
+SCRATCH = {
+    "idout": ("dram", [128, 3], "bfloat16"),
+    "idin": ("dram", [N, 128, 3], "bfloat16"),
+    "tgb": ("sbuf", [128, 3 * NC], "bfloat16"),
+    "rm": ("sbuf", [128, 3 * NC], "bfloat16"),
+    "rl": ("sbuf", [128, 3 * NC], "bfloat16"),
+    "kt": ("sbuf", [128, 9 * NC], "bfloat16"),
+    "km": ("sbuf", [128, NC], "bfloat16"),
+    "kl": ("sbuf", [128, NC], "bfloat16"),
+    "kb": ("sbuf", [128, N * NC], "bfloat16"),
+    "idx": ("sbuf", [128, 4], "bfloat16"),
+    "tabb": ("sbuf", [128, 2048], "bfloat16"),
+    "ct": ("sbuf", [128, 512], MX), "st": ("sbuf", [128, 512], "uint8"),
+    "wb": ("sbuf", [128, 512], "bfloat16"),
+    "cw": ("sbuf", [128, 128], MX), "sw": ("sbuf", [128, 128], "uint8"),
+    "o": ("sbuf", [128, 4 * N * NC], "bfloat16"),
+    "co": ("sbuf", [128, N * NC], MX), "so": ("sbuf", [128, N * NC], "uint8"),
+    "e": ("sbuf", [128, 4 * N * NC], "bfloat16"),
+    "ce": ("sbuf", [128, N * NC], MX), "se": ("sbuf", [128, N * NC], "uint8"),
+    "cl": ("sbuf", [128, N * NC], MX), "sl": ("sbuf", [128, N * NC], "uint8"),
+    "rc": ("sbuf", [128, 2 * NC], MX), "rs": ("sbuf", [128, 2 * NC], "uint8"),
+    "ysb": ("sbuf", [128, NC], "float32"),
+    "z": ("psum", [128, 8 * 512], "float32"),
+}
+SEMAPHORES = (["ldst", "ldtg", "ldtab", "ldw", "rowm", "rowl", "styy", "iot", "ms", "qt", "qw", "ymm", "ycp", "lsem"]
+              + ["idin%d" % j for j in range(N)] + ["ein%d" % j for j in range(N)]
+              + ["rc%d" % k for k in range(2)] + ["rs%d" % k for k in range(2)]
+              + ["%s%d" % (n, k) for n in ("ka", "ku", "kk") for k in range(3)]
+              + ["%s%d" % (n, k) for n in ("bc", "oh", "qo", "cp", "qe") for k in range(4)]
+              + ["mm%d%d" % (k, f) for k in range(4) for f in range(4)])
+
+
+def bits(mask):
+    return [1 << i for i in range(16) if (mask >> i) & 1]
+
+
+def share(engines, k):
+    size = 1
+    while size * 2 * k <= len(engines):
+        size *= 2
+    extra, pos, out = (len(engines) - size * k) // size, 0, []
+    for i in range(k):
+        n = size * 2 if i < extra else size
+        out.append(sum(engines[pos:pos + n]))
+        pos += n
+    return out
+
+
+def deal(topo, src, dsts):
+    off = [d for d in dsts if topo.chip(d) != topo.chip(src)]
+    on = [d for d in dsts if topo.chip(d) == topo.chip(src)]
+    got = {}
+    free = None
+    if on:
+        free = bits(topo.mask(src, on[0]))
+    if off:
+        eng = bits(topo.mask(src, off[0]))
+        got.update(zip(off, share(eng, len(off))))
+        if on:
+            free = [b for b in free if b not in eng]
+    if on:
+        got.update(zip(on, share(free, len(on))))
+    return [got[d] for d in dsts]
+
+
+def count(mask):
+    return len(bits(mask))
+
+
+def make_plan(T, topo):
+    C = list(T.cores)
+    may = topo.may_write
+    need = [[d for d in range(N) if d != j and not may(C[j], C[d])] for j in range(N)]
+    relay, relay_jobs, id_relay, id_partner = {}, {}, {}, {}
+    for j in range(N):
+        if not need[j]:
+            continue
+        xs = [x for x in range(128) if topo.chip(x) == topo.chip(C[j]) and topo.die(x) == topo.die(C[j]) and x not in C
+              and all(may(x, C[d]) for d in need[j])]
+        partner = [q for q in range(N) if q != j and topo.chip(C[q]) == topo.chip(C[j])
+                   and all(may(C[q], C[d]) for d in need[j])][0]
+        direct_back = [d for d in need[j] if may(C[d], C[j])]
+        both = [d for d in need[j] if d not in direct_back]
+        for part in (direct_back, both):
+            for k, d in enumerate(part):
+                x = xs[k % len(xs)]
+                jobs = relay_jobs.setdefault(x, [])
+                relay[j, d] = (x, len(jobs))
+                jobs.append((j, d))
+        for d in direct_back:
+            id_relay[j, d] = relay[j, d][0]
+        for d in both:
+            id_partner[j, d] = partner
+    late = [[j for j in range(N) if r in need[j]] for r in range(N)]
+
+    def far(r, d):
+        if d in need[r]:
+            return 0
+        if topo.chip(C[d]) == topo.chip(C[r]):
+            return 3
+        return 2 if topo.same_plane(topo.chip(C[d]), topo.chip(C[r])) else 1
+    mid = [sorted([j for j in range(N) if j != r and j not in late[r]], key=lambda d: far(r, d)) for r in range(N)]
+
+    idcalls = {}
+    for j in range(N):
+        direct = [d for d in range(N) if d != j and may(C[j], C[d])]
+        calls = []
+        if not need[j]:
+            on = [C[d] for d in direct if topo.chip(C[d]) == topo.chip(C[j])]
+            off = [C[d] for d in direct if topo.chip(C[d]) != topo.chip(C[j])]
+            calls.append([(bits(topo.mask(C[j], on[0]))[-1], on), (bits(topo.mask(C[j], off[0]))[0], off)])
+        else:
+            first = [C[q] for q in sorted(set(id_partner[j, d] for d in need[j] if (j, d) in id_partner))]
+            rest = [id_relay[j, d] for d in need[j] if (j, d) in id_relay] + [C[d] for d in direct]
+            rest = [c for k, c in enumerate(rest) if c not in first and c not in rest[:k]]
+            calls.append([(bits(topo.mask(C[j], c))[-1 - k], [c]) for k, c in enumerate(first)])
+            calls.append([(m, [c]) for m, c in zip(deal(topo, C[j], rest), rest)])
+        for call in calls:
+            idcalls.setdefault(C[j], []).append((j, call))
+    for (j, d), q in sorted(id_partner.items()):
+        got = [v for v in idcalls[C[q]] if v[0] == j]
+        if got:
+            continue
+        ds = [C[x] for x in range(N) if id_partner.get((j, x)) == q]
+        idcalls[C[q]].append((j, [(m, [c]) for m, c in zip([bits(topo.mask(C[q], c))[1 + k] for k, c in enumerate(ds)], ds)]))
+    for (j, d), x in sorted(id_relay.items()):
+        idcalls.setdefault(x, []).append((j, [(topo.mask(x, C[d]), [C[d]])]))
+    idcount = {}
+    for calls in idcalls.values():
+        for j, call in calls:
+            for m, ds in call:
+                for c in ds:
+                    idcount[c, j] = idcount.get((c, j), 0) + count(m)
+
+    rounds = []
+    for r in range(N):
+        rr = []
+        for ds in (mid[r], late[r]):
+            hop = [relay[r, d][0] if (r, d) in relay else C[d] for d in ds]
+            rr.append(list(zip(ds, hop, deal(topo, C[r], hop))))
+        rounds.append(rr)
+    return dict(C=C, need=need, late=late, mid=mid, relay=relay, relay_jobs=relay_jobs, id_relay=id_relay, id_partner=id_partner,
+                idcalls=idcalls, idcount=idcount, rounds=rounds)
+
+
+def dst_id(topo, c):
+    a = topo.addr(c)
+    return DstId(rid=a[0], pnc=a[1])
+
+
+def send_ids(g, T, topo, P, core, j, call, own):
+    src = T.idout[:] if own else T.idin[j]
+    g.remote_dma_fused([RemoteDMATransfer(dst_ids=[dst_id(topo, c) for c in ds], dma_engine_mask=m, remote_sem=T.sem["idin%d" % j],
+                                          srcs=[src], dsts=[T.idin[j] for c in ds]) for m, ds in call], local_sem=T.sem.lsem)
+    return sum(count(m) for m, ds in call)
+
+
+def relay_program(g, core, T, topo, P):
+    sent = 0
+    for j, call in P["idcalls"].get(core, []):
+        g.wait_ge(T.sem["idin%d" % j], P["idcount"][core, j])
+        sent += send_ids(g, T, topo, P, core, j, call, False)
+    for k, (j, d) in enumerate(P["relay_jobs"][core]):
+        c = P["C"][d]
+        m1 = [m for rnd in P["rounds"][j] for dd, hop, m in rnd if dd == d][0]
+        m2 = topo.mask(core, c)
+        rid, pid = topo.addr(c)[0], topo.addr(c)[1]
+        lo, hi = k * NC, (k + 1) * NC
+        g.wait_ge(T.sem["rc%d" % k], count(m1))
+        g.remote_dma(T.cl[:, j * NC:(j + 1) * NC].bitcast(dt.uint8), T.rc[:, lo:hi].bitcast(dt.uint8),
+                     T.sem["ein%d" % j], T.sem.lsem, pid, rid, m2)
+        g.wait_ge(T.sem["rs%d" % k], count(m1))
+        g.remote_dma(T.sl[:, j * NC:(j + 1) * NC], T.rs[:, lo:hi], T.sem["ein%d" % j], T.sem.lsem, pid, rid, m2)
+        sent += 2 * count(m2)
+    g.wait_ge(T.sem.lsem, sent)
+
+
+def rank_program(g, core, T, topo):
+    P = make_plan(T, topo)
+    me = T.rank_of(core)
+    if me is None:
+        if core in P["relay_jobs"]:
+            relay_program(g, core, T, topo, P)
+        return
+    C, mid, late = P["C"], P["mid"][me], P["late"][me]
+    relayed = bool(P["need"][me])
+    order = [me] + mid + late
+    nm = len(mid)
+    cut = [(0, 1), (1, 3), (3, 1 + nm), (1 + nm, N)]
+    S = T.sem
+    V, A, PE, SY = g.vector, g.scalar, g.tensor, g.sync
+    OP = AluOpType
+
+    SY.dma_start(T.idout[:], T.tg[0:1, :]).then_inc(S.ldst, 16)
+    SY.dma_start(T.tgb[:], T.tg[:]).then_inc(S.ldtg, 16)
+    SY.dma_start(T.tabb[:], T.tab[:]).then_inc(S.ldtab, 16)
+    SY.dma_start(T.wb[:], T.w[:]).then_inc(S.ldw, 16)
+    SY.wait_ge(S.ms, 2)
+    for ranks, buf, sem in ((mid, T.rm, S.rowm), (late, T.rl, S.rowl)):
+        for i in reversed(range(len(ranks))):
+            j = ranks[i]
+            SY.wait_ge(S["idin%d" % j], P["idcount"][core, j])
+            SY.dma_start(buf[32 * i:32 * i + 1, :], T.idin[j]).then_inc(sem, 16)
+
+    rows_m, rows_l = 32 * (nm - 1) + 1, 32 * (len(late) - 1) + 1
+    V.memset(T.rm[0:rows_m, :], 0.0).then_inc(S.ms, 1)
+    V.memset(T.rl[0:rows_l, :], 0.0).then_inc(S.ms, 1)
+
+    def keys(q, x, out, n):
+        a, t, u = [T.kt[0:n, (3 * q + i) * NC:(3 * q + i + 1) * NC] for i in range(3)]
+        V.tensor_scalar(a, x[0:n, 0:NC], float(me), 1024.0, OP.not_equal, OP.mult).then_inc(S["ka%d" % q], 1)
+        V.tensor_scalar(t, x[0:n, NC:2 * NC], 4.0, -256.0, OP.mult, OP.add).then_inc(S["ka%d" % q], 1)
+        V.wait_ge(S["ka%d" % q], 2)
+        V.tensor_tensor(u, t, x[0:n, 2 * NC:3 * NC], OP.add).then_inc(S["ku%d" % q], 1)
+        V.wait_ge(S["ku%d" % q], 1)
+        V.tensor_tensor(out, u, a, OP.add).then_inc(S["kk%d" % q], 1)
+
+    def onehots(k):
+        lo, hi = cut[k]
+        for b in range(4):
+            V.tensor_scalar(T.o[:, 4 * NC * lo + b:4 * NC * hi:4], T.kb[:, NC * lo:NC * hi], T.idx[:, b:b + 1], None,
+                            OP.is_equal).then_inc(S["oh%d" % k], 1)
+        V.wait_ge(S["oh%d" % k], 4)
+        V.quantize_mx(T.co[:, NC * lo:NC * hi], T.so[:, NC * lo:NC * hi], T.o[:, 4 * NC * lo:4 * NC * hi]).then_inc(S["qo%d" % k], 1)
+
+    def bank(k, f):
+        return 512 * (4 * (k % 2) + f)
+
+    def products(k):
+        lo, hi = cut[k]
+        PE.wait_ge(S["qo%d" % k], 1)
+        if k >= 2:
+            PE.wait_ge(S["cp%d" % (k - 2)], 4)
+        for f in range(4):
+            PE.matmul_mx(T.z[:, bank(k, f):bank(k, f) + NC * (hi - lo)], T.ct[:, 128 * f:128 * f + 128], T.st[:, 128 * f:128 * f + 128],
+                         T.co[:, NC * lo:NC * hi], T.so[:, NC * lo:NC * hi], True, True).then_inc(S["mm%d%d" % (k, f)], 1)
+
+    def views(k, f):
+        lo, hi = cut[k]
+        return T.e[:, 4 * NC * lo + f:4 * NC * hi:4], T.z[:, bank(k, f):bank(k, f) + NC * (hi - lo)]
+
+    def entries(k):
+        lo, hi = cut[k]
+        for f in (0, 1):
+            V.wait_ge(S["mm%d%d" % (k, f)], 1)
+            out, in_ = views(k, f)
+            V.tensor_copy(out, in_).then_inc(S["cp%d" % k], 1)
+        V.wait_ge(S["cp%d" % k], 4)
+        V.quantize_mx(T.ce[:, NC * lo:NC * hi], T.se[:, NC * lo:NC * hi], T.e[:, 4 * NC * lo:4 * NC * hi]).then_inc(S["qe%d" % k], 1)
+
+    V.wait_ge(S.ldtg, 16)
+    keys(0, T.tgb, T.kb[:, 0:NC], 128)
+    V.wait_ge(S.kk0, 1)
+    V.wait_ge(S.iot, 1)
+    onehots(0)
+    V.wait_ge(S.ldtab, 16)
+    V.quantize_mx(T.ct[:], T.st[:], T.tabb[:]).then_inc(S.qt, 1)
+    V.wait_ge(S.ldw, 16)
+    V.quantize_mx(T.cw[:], T.sw[:], T.wb[:]).then_inc(S.qw, 1)
+    entries(0)
+    V.wait_ge(S.rowm, 16 * nm)
+    keys(1, T.rm, T.km[0:rows_m, :], rows_m)
+    V.wait_ge(S.bc1, 2)
+    onehots(1)
+    entries(1)
+    V.wait_ge(S.bc2, nm - 2)
+    onehots(2)
+    if not relayed:
+        entries(2)
+    V.wait_ge(S.rowl, 16 * len(late))
+    keys(2, T.rl, T.kl[0:rows_l, :], rows_l)
+    if relayed:
+        entries(2)
+    V.wait_ge(S.bc3, len(late))
+    onehots(3)
+    entries(3)
+
+    for k in range(4):
+        for f in (2, 3):
+            A.wait_ge(S["mm%d%d" % (k, f)], 1)
+            out, in_ = views(k, f)
+            A.activation(out, in_, ActivationFunctionType.Copy).then_inc(S["cp%d" % k], 1)
+
+    PE.wait_ge(S.qt, 1)
+    for k in range(4):
+        products(k)
+    def hops(r):
+        there = 2.5 if (me, r) in P["id_relay"] else 2 if (me, r) in P["id_partner"] else 1
+        back = 2 if (r, me) in P["relay"] else 1
+        return there + back - (0.5 if topo.chip(C[r]) == topo.chip(core) else 0)
+    others = sorted([r for r in range(N) if r != me], key=hops)
+    PE.wait_ge(S.cp2, 4)
+    PE.wait_ge(S.qe0, 1)
+    PE.wait_ge(S.qw, 1)
+    ybank = T.z[:, 0:NC]
+    PE.matmul_mx(ybank, T.cw[:], T.sw[:], T.ce[:, 0:NC], T.se[:, 0:NC], True, False)
+    for i, r in enumerate(others):
+        if (r, me) in P["relay"]:
+            n = count(topo.mask(P["relay"][r, me][0], core))
+        else:
+            n = [count(m) for rnd in P["rounds"][r] for d, hop, m in rnd if d == me][0]
+        PE.wait_ge(S["ein%d" % r], 2 * n)
+        mm = PE.matmul_mx(ybank, T.cw[:], T.sw[:], T.cl[:, r * NC:(r + 1) * NC], T.sl[:, r * NC:(r + 1) * NC], False, i == N - 2)
+    mm.then_inc(S.ymm, 1)
+    A.wait_ge(S.ymm, 1)
+    A.activation(T.ysb[:], ybank, ActivationFunctionType.Copy).then_inc(S.ycp, 1)
+    SY.wait_ge(S.ycp, 1)
+    SY.dma_start(T.y[:], T.ysb[:]).then_inc(S.styy, 16)
+    SY.wait_ge(S.styy, 16)
+
+    sent = 0
+    g.iota(T.idx[:], [[1, 4]], -256, 4, allow_small_or_imprecise_dtypes=True).then_inc(S.iot, 1)
+    g.wait_ge(S.ldst, 16)
+    for j, call in P["idcalls"][core]:
+        if j != me:
+            g.wait_ge(S["idin%d" % j], P["idcount"][core, j])
+        sent += send_ids(g, T, topo, P, core, j, call, j == me)
+
+    def spread_keys(q, src, n, first):
+        g.wait_ge(S["kk%d" % q], 1)
+        for i in range(n):
+            s = first + i
+            k = 3 if q == 2 else (1 if s < 3 else 2)
+            g.partition_broadcast(T.kb[:, NC * s:NC * (s + 1)], src[32 * i:32 * i + 1, :], 128).then_inc(S["bc%d" % k], 1)
+
+    def send_round(n):
+        out = 0
+        for c, s in ((True, False), (False, True)):
+            ts = []
+            for d, hop, m in P["rounds"][me][n]:
+                b = order.index(d)
+                lo, hi = NC * b, NC * (b + 1)
+                if (me, d) in P["relay"]:
+                    k = P["relay"][me, d][1]
+                    land, sem = (T.rc if c else T.rs)[:, NC * k:NC * (k + 1)], S["%s%d" % ("rc" if c else "rs", k)]
+                else:
+                    land, sem = (T.cl if c else T.sl)[:, NC * me:NC * (me + 1)], S["ein%d" % me]
+                src = (T.ce if c else T.se)[:, lo:hi]
+                if c:
+                    src, land = src.bitcast(dt.uint8), land.bitcast(dt.uint8)
+                ts.append(RemoteDMATransfer(dst_ids=[dst_id(topo, hop)], dma_engine_mask=m, remote_sem=sem, srcs=[src], dsts=[land]))
+                out += count(m)
+            g.remote_dma_fused(ts, local_sem=S.lsem)
+        return out
+
+    spread_keys(1, T.km, nm, 1)
+    if relayed:
+        spread_keys(2, T.kl, len(late), 1 + nm)
+    g.wait_ge(S.qe1, 1)
+    g.wait_ge(S.qe2, 1)
+    sent += send_round(0)
+    if not relayed:
+        spread_keys(2, T.kl, len(late), 1 + nm)
+    g.wait_ge(S.qe3, 1)
+    sent += send_round(1)
+    g.wait_ge(S.lsem, sent)

@@ -33,12 +33,16 @@ SEMAPHORES = (["ldst", "ldtg", "ldtab", "ldw", "rowm", "rowl", "styy", "iot", "m
               + ["idin%d" % j for j in range(N)] + ["ein%d" % j for j in range(N)]
               + ["rc%d" % k for k in range(2)] + ["rs%d" % k for k in range(2)]
               + ["%s%d" % (n, k) for n in ("ka", "ku", "kk") for k in range(3)]
-              + ["%s%d" % (n, k) for n in ("bc", "oh", "qo", "cp", "qe") for k in range(4)]
-              + ["mm%d%d" % (k, f) for k in range(4) for f in range(4)])
+              + ["%s%d" % (n, k) for n in ("bc", "oh", "qo", "cp", "qe") for k in range(N)]
+              + ["mm%d%d" % (k, f) for k in range(N) for f in range(4)])
 
 
 def bits(mask):
     return [1 << i for i in range(16) if (mask >> i) & 1]
+
+
+def count(mask):
+    return len(bits(mask))
 
 
 def share(engines, k):
@@ -56,8 +60,7 @@ def share(engines, k):
 def deal(topo, src, dsts):
     off = [d for d in dsts if topo.chip(d) != topo.chip(src)]
     on = [d for d in dsts if topo.chip(d) == topo.chip(src)]
-    got = {}
-    free = None
+    got, free = {}, None
     if on:
         free = bits(topo.mask(src, on[0]))
     if off:
@@ -68,10 +71,6 @@ def deal(topo, src, dsts):
     if on:
         got.update(zip(on, share(free, len(on))))
     return [got[d] for d in dsts]
-
-
-def count(mask):
-    return len(bits(mask))
 
 
 def make_plan(T, topo):
@@ -118,18 +117,17 @@ def make_plan(T, topo):
             calls.append([(bits(topo.mask(C[j], on[0]))[-1], on), (bits(topo.mask(C[j], off[0]))[0], off)])
         else:
             first = [C[q] for q in sorted(set(id_partner[j, d] for d in need[j] if (j, d) in id_partner))]
-            rest = [id_relay[j, d] for d in need[j] if (j, d) in id_relay] + [C[d] for d in direct]
-            rest = [c for k, c in enumerate(rest) if c not in first and c not in rest[:k]]
+            first += sorted(set(id_relay[j, d] for d in need[j] if (j, d) in id_relay))
+            rest = [C[d] for d in direct if C[d] not in first]
             calls.append([(bits(topo.mask(C[j], c))[-1 - k], [c]) for k, c in enumerate(first)])
-            calls.append([(m, [c]) for m, c in zip(deal(topo, C[j], rest), rest)])
+            if rest:
+                calls.append([(m, [c]) for m, c in zip(deal(topo, C[j], rest), rest)])
         for call in calls:
             idcalls.setdefault(C[j], []).append((j, call))
     for (j, d), q in sorted(id_partner.items()):
-        got = [v for v in idcalls[C[q]] if v[0] == j]
-        if got:
-            continue
-        ds = [C[x] for x in range(N) if id_partner.get((j, x)) == q]
-        idcalls[C[q]].append((j, [(m, [c]) for m, c in zip([bits(topo.mask(C[q], c))[1 + k] for k, c in enumerate(ds)], ds)]))
+        if not [v for v in idcalls[C[q]] if v[0] == j]:
+            ds = [C[x] for x in range(N) if id_partner.get((j, x)) == q]
+            idcalls[C[q]].append((j, [(bits(topo.mask(C[q], c))[1 + k], [c]) for k, c in enumerate(ds)]))
     for (j, d), x in sorted(id_relay.items()):
         idcalls.setdefault(x, []).append((j, [(topo.mask(x, C[d]), [C[d]])]))
     idcount = {}
@@ -139,15 +137,25 @@ def make_plan(T, topo):
                 for c in ds:
                     idcount[c, j] = idcount.get((c, j), 0) + count(m)
 
-    rounds = []
+    seq, rounds, ecount = [], [], {}
     for r in range(N):
+        m, l = mid[r], late[r]
+        if need[r]:
+            seq.append(m[:2] + l + m[2:])
+            groups = [m[:2], l, m[2:]]
+        else:
+            seq.append(m + l)
+            groups = [m[:2], m[2:], l] if len(m) > 3 else [m[:2], m[2:] + l]
         rr = []
-        for ds in (mid[r], late[r]):
+        for ds in groups:
             hop = [relay[r, d][0] if (r, d) in relay else C[d] for d in ds]
             rr.append(list(zip(ds, hop, deal(topo, C[r], hop))))
         rounds.append(rr)
-    return dict(C=C, need=need, late=late, mid=mid, relay=relay, relay_jobs=relay_jobs, id_relay=id_relay, id_partner=id_partner,
-                idcalls=idcalls, idcount=idcount, rounds=rounds)
+        for rnd in rr:
+            for d, hop, mask in rnd:
+                ecount[r, d] = 2 * count(topo.mask(hop, C[d]) if (r, d) in relay else mask)
+    return dict(C=C, late=late, mid=mid, relay=relay, relay_jobs=relay_jobs, id_relay=id_relay, id_partner=id_partner,
+                idcalls=idcalls, idcount=idcount, seq=seq, rounds=rounds, ecount=ecount)
 
 
 def dst_id(topo, c):
@@ -155,7 +163,7 @@ def dst_id(topo, c):
     return DstId(rid=a[0], pnc=a[1])
 
 
-def send_ids(g, T, topo, P, core, j, call, own):
+def send_ids(g, T, topo, j, call, own):
     src = T.idout[:] if own else T.idin[j]
     g.remote_dma_fused([RemoteDMATransfer(dst_ids=[dst_id(topo, c) for c in ds], dma_engine_mask=m, remote_sem=T.sem["idin%d" % j],
                                           srcs=[src], dsts=[T.idin[j] for c in ds]) for m, ds in call], local_sem=T.sem.lsem)
@@ -166,7 +174,7 @@ def relay_program(g, core, T, topo, P):
     sent = 0
     for j, call in P["idcalls"].get(core, []):
         g.wait_ge(T.sem["idin%d" % j], P["idcount"][core, j])
-        sent += send_ids(g, T, topo, P, core, j, call, False)
+        sent += send_ids(g, T, topo, j, call, False)
     for k, (j, d) in enumerate(P["relay_jobs"][core]):
         c = P["C"][d]
         m1 = [m for rnd in P["rounds"][j] for dd, hop, m in rnd if dd == d][0]
@@ -190,10 +198,9 @@ def rank_program(g, core, T, topo):
             relay_program(g, core, T, topo, P)
         return
     C, mid, late = P["C"], P["mid"][me], P["late"][me]
-    relayed = bool(P["need"][me])
-    order = [me] + mid + late
+    order = [me] + P["seq"][me]
+    kl = order.index(late[0])
     nm = len(mid)
-    cut = [(0, 1), (1, 3), (3, 1 + nm), (1 + nm, N)]
     S = T.sem
     V, A, PE, SY = g.vector, g.scalar, g.tensor, g.sync
     OP = AluOpType
@@ -223,37 +230,38 @@ def rank_program(g, core, T, topo):
         V.tensor_tensor(out, u, a, OP.add).then_inc(S["kk%d" % q], 1)
 
     def onehots(k):
-        lo, hi = cut[k]
+        lo, hi = NC * k, NC * (k + 1)
         for b in range(4):
-            V.tensor_scalar(T.o[:, 4 * NC * lo + b:4 * NC * hi:4], T.kb[:, NC * lo:NC * hi], T.idx[:, b:b + 1], None,
-                            OP.is_equal).then_inc(S["oh%d" % k], 1)
+            V.tensor_scalar(T.o[:, 4 * lo + b:4 * hi:4], T.kb[:, lo:hi], T.idx[:, b:b + 1], None, OP.is_equal).then_inc(S["oh%d" % k], 1)
         V.wait_ge(S["oh%d" % k], 4)
-        V.quantize_mx(T.co[:, NC * lo:NC * hi], T.so[:, NC * lo:NC * hi], T.o[:, 4 * NC * lo:4 * NC * hi]).then_inc(S["qo%d" % k], 1)
+        V.quantize_mx(T.co[:, lo:hi], T.so[:, lo:hi], T.o[:, 4 * lo:4 * hi]).then_inc(S["qo%d" % k], 1)
 
     def bank(k, f):
-        return 512 * (4 * (k % 2) + f)
+        at = 512 * (4 * (k % 2) + f)
+        return T.z[:, at:at + NC]
 
     def products(k):
-        lo, hi = cut[k]
+        lo, hi = NC * k, NC * (k + 1)
         PE.wait_ge(S["qo%d" % k], 1)
         if k >= 2:
             PE.wait_ge(S["cp%d" % (k - 2)], 4)
         for f in range(4):
-            PE.matmul_mx(T.z[:, bank(k, f):bank(k, f) + NC * (hi - lo)], T.ct[:, 128 * f:128 * f + 128], T.st[:, 128 * f:128 * f + 128],
-                         T.co[:, NC * lo:NC * hi], T.so[:, NC * lo:NC * hi], True, True).then_inc(S["mm%d%d" % (k, f)], 1)
+            PE.matmul_mx(bank(k, f), T.ct[:, NC * f:NC * (f + 1)], T.st[:, NC * f:NC * (f + 1)],
+                         T.co[:, lo:hi], T.so[:, lo:hi], True, True).then_inc(S["mm%d%d" % (k, f)], 1)
 
-    def views(k, f):
-        lo, hi = cut[k]
-        return T.e[:, 4 * NC * lo + f:4 * NC * hi:4], T.z[:, bank(k, f):bank(k, f) + NC * (hi - lo)]
+    def by_vector(k):
+        return (0, 1) if k == N - 1 else ()
+
+    def e_view(k, f):
+        return T.e[:, 4 * NC * k + f:4 * NC * (k + 1):4]
 
     def entries(k):
-        lo, hi = cut[k]
-        for f in (0, 1):
+        lo, hi = NC * k, NC * (k + 1)
+        for f in by_vector(k):
             V.wait_ge(S["mm%d%d" % (k, f)], 1)
-            out, in_ = views(k, f)
-            V.tensor_copy(out, in_).then_inc(S["cp%d" % k], 1)
+            V.tensor_copy(e_view(k, f), bank(k, f)).then_inc(S["cp%d" % k], 1)
         V.wait_ge(S["cp%d" % k], 4)
-        V.quantize_mx(T.ce[:, NC * lo:NC * hi], T.se[:, NC * lo:NC * hi], T.e[:, 4 * NC * lo:4 * NC * hi]).then_inc(S["qe%d" % k], 1)
+        V.quantize_mx(T.ce[:, lo:hi], T.se[:, lo:hi], T.e[:, 4 * lo:4 * hi]).then_inc(S["qe%d" % k], 1)
 
     V.wait_ge(S.ldtg, 16)
     keys(0, T.tgb, T.kb[:, 0:NC], 128)
@@ -267,46 +275,38 @@ def rank_program(g, core, T, topo):
     entries(0)
     V.wait_ge(S.rowm, 16 * nm)
     keys(1, T.rm, T.km[0:rows_m, :], rows_m)
-    V.wait_ge(S.bc1, 2)
-    onehots(1)
-    entries(1)
-    V.wait_ge(S.bc2, nm - 2)
-    onehots(2)
-    if not relayed:
-        entries(2)
-    V.wait_ge(S.rowl, 16 * len(late))
-    keys(2, T.rl, T.kl[0:rows_l, :], rows_l)
-    if relayed:
-        entries(2)
-    V.wait_ge(S.bc3, len(late))
-    onehots(3)
-    entries(3)
+    for k in range(1, N):
+        if k == kl - 1:
+            V.wait_ge(S.rowl, 16 * len(late))
+            keys(2, T.rl, T.kl[0:rows_l, :], rows_l)
+        V.wait_ge(S["bc%d" % k], 1)
+        onehots(k)
+        if k > 1:
+            entries(k - 1)
+    entries(N - 1)
 
-    for k in range(4):
-        for f in (2, 3):
-            A.wait_ge(S["mm%d%d" % (k, f)], 1)
-            out, in_ = views(k, f)
-            A.activation(out, in_, ActivationFunctionType.Copy).then_inc(S["cp%d" % k], 1)
+    for k in range(N):
+        for f in range(4):
+            if f not in by_vector(k):
+                A.wait_ge(S["mm%d%d" % (k, f)], 1)
+                A.activation(e_view(k, f), bank(k, f), ActivationFunctionType.Copy).then_inc(S["cp%d" % k], 1)
 
     PE.wait_ge(S.qt, 1)
-    for k in range(4):
+    for k in range(N):
         products(k)
+
     def hops(r):
         there = 2.5 if (me, r) in P["id_relay"] else 2 if (me, r) in P["id_partner"] else 1
         back = 2 if (r, me) in P["relay"] else 1
         return there + back - (0.5 if topo.chip(C[r]) == topo.chip(core) else 0)
     others = sorted([r for r in range(N) if r != me], key=hops)
-    PE.wait_ge(S.cp2, 4)
+    PE.wait_ge(S["cp%d" % (N - 2)], 4)
     PE.wait_ge(S.qe0, 1)
     PE.wait_ge(S.qw, 1)
-    ybank = T.z[:, 0:NC]
+    ybank = bank(N - 2, 0)
     PE.matmul_mx(ybank, T.cw[:], T.sw[:], T.ce[:, 0:NC], T.se[:, 0:NC], True, False)
     for i, r in enumerate(others):
-        if (r, me) in P["relay"]:
-            n = count(topo.mask(P["relay"][r, me][0], core))
-        else:
-            n = [count(m) for rnd in P["rounds"][r] for d, hop, m in rnd if d == me][0]
-        PE.wait_ge(S["ein%d" % r], 2 * n)
+        PE.wait_ge(S["ein%d" % r], P["ecount"][r, me])
         mm = PE.matmul_mx(ybank, T.cw[:], T.sw[:], T.cl[:, r * NC:(r + 1) * NC], T.sl[:, r * NC:(r + 1) * NC], False, i == N - 2)
     mm.then_inc(S.ymm, 1)
     A.wait_ge(S.ymm, 1)
@@ -321,43 +321,31 @@ def rank_program(g, core, T, topo):
     for j, call in P["idcalls"][core]:
         if j != me:
             g.wait_ge(S["idin%d" % j], P["idcount"][core, j])
-        sent += send_ids(g, T, topo, P, core, j, call, j == me)
+        sent += send_ids(g, T, topo, j, call, j == me)
 
-    def spread_keys(q, src, n, first):
-        g.wait_ge(S["kk%d" % q], 1)
-        for i in range(n):
-            s = first + i
-            k = 3 if q == 2 else (1 if s < 3 else 2)
-            g.partition_broadcast(T.kb[:, NC * s:NC * (s + 1)], src[32 * i:32 * i + 1, :], 128).then_inc(S["bc%d" % k], 1)
+    for k in range(1, N):
+        j = order[k]
+        src, i, kk = (T.km, mid.index(j), S.kk1) if j in mid else (T.kl, late.index(j), S.kk2)
+        g.wait_ge(kk, 1)
+        g.partition_broadcast(T.kb[:, NC * k:NC * (k + 1)], src[32 * i:32 * i + 1, :], 128).then_inc(S["bc%d" % k], 1)
 
-    def send_round(n):
-        out = 0
-        for c, s in ((True, False), (False, True)):
+    for rnd in P["rounds"][me]:
+        for d, hop, m in rnd:
+            g.wait_ge(S["qe%d" % order.index(d)], 1)
+        for c in (True, False):
             ts = []
-            for d, hop, m in P["rounds"][me][n]:
-                b = order.index(d)
-                lo, hi = NC * b, NC * (b + 1)
+            for d, hop, m in rnd:
+                k = order.index(d)
+                lo, hi = NC * k, NC * (k + 1)
                 if (me, d) in P["relay"]:
-                    k = P["relay"][me, d][1]
-                    land, sem = (T.rc if c else T.rs)[:, NC * k:NC * (k + 1)], S["%s%d" % ("rc" if c else "rs", k)]
+                    q = P["relay"][me, d][1]
+                    land, sem = (T.rc if c else T.rs)[:, NC * q:NC * (q + 1)], S["%s%d" % ("rc" if c else "rs", q)]
                 else:
                     land, sem = (T.cl if c else T.sl)[:, NC * me:NC * (me + 1)], S["ein%d" % me]
                 src = (T.ce if c else T.se)[:, lo:hi]
                 if c:
                     src, land = src.bitcast(dt.uint8), land.bitcast(dt.uint8)
                 ts.append(RemoteDMATransfer(dst_ids=[dst_id(topo, hop)], dma_engine_mask=m, remote_sem=sem, srcs=[src], dsts=[land]))
-                out += count(m)
+                sent += count(m)
             g.remote_dma_fused(ts, local_sem=S.lsem)
-        return out
-
-    spread_keys(1, T.km, nm, 1)
-    if relayed:
-        spread_keys(2, T.kl, len(late), 1 + nm)
-    g.wait_ge(S.qe1, 1)
-    g.wait_ge(S.qe2, 1)
-    sent += send_round(0)
-    if not relayed:
-        spread_keys(2, T.kl, len(late), 1 + nm)
-    g.wait_ge(S.qe3, 1)
-    sent += send_round(1)
     g.wait_ge(S.lsem, sent)

@@ -11,10 +11,13 @@ SCRATCH = {
     "tgb": ("sbuf", [128, 3 * NC], "bfloat16"),
     "rm": ("sbuf", [128, 3 * NC], "bfloat16"),
     "rl": ("sbuf", [128, 3 * NC], "bfloat16"),
-    "kt": ("sbuf", [128, 9 * NC], "bfloat16"),
+    "kt": ("sbuf", [128, 6 * NC], "bfloat16"),
     "km": ("sbuf", [128, NC], "bfloat16"),
     "kl": ("sbuf", [128, NC], "bfloat16"),
+    "ko": ("sbuf", [128, 2 * NC], "bfloat16"),
+    "kx": ("sbuf", [128, 5 * NC], "bfloat16"),
     "kb": ("sbuf", [128, N * NC], "bfloat16"),
+    "kq": ("sbuf", [128, 4 * NC], "bfloat16"),
     "idx": ("sbuf", [128, 4], "bfloat16"),
     "tabb": ("sbuf", [128, 2048], "bfloat16"),
     "ct": ("sbuf", [128, 512], MX), "st": ("sbuf", [128, 512], "uint8"),
@@ -22,17 +25,22 @@ SCRATCH = {
     "cw": ("sbuf", [128, 128], MX), "sw": ("sbuf", [128, 128], "uint8"),
     "o": ("sbuf", [128, 4 * N * NC], "bfloat16"),
     "co": ("sbuf", [128, N * NC], MX), "so": ("sbuf", [128, N * NC], "uint8"),
+    "oq": ("sbuf", [128, 4 * 4 * NC], "bfloat16"),
+    "cq": ("sbuf", [128, 4 * NC], MX), "sq": ("sbuf", [128, 4 * NC], "uint8"),
+    "qcl": ("sbuf", [128, NC], MX), "qsl": ("sbuf", [128, NC], "uint8"),
     "e": ("sbuf", [128, 4 * N * NC], "bfloat16"),
     "ce": ("sbuf", [128, N * NC], MX), "se": ("sbuf", [128, N * NC], "uint8"),
     "cl": ("sbuf", [128, N * NC], MX), "sl": ("sbuf", [128, N * NC], "uint8"),
-    "rc": ("sbuf", [128, 2 * NC], MX), "rs": ("sbuf", [128, 2 * NC], "uint8"),
+    "rc": ("sbuf", [128, 4 * NC], MX), "rs": ("sbuf", [128, 4 * NC], "uint8"),
     "ysb": ("sbuf", [128, NC], "float32"),
     "z": ("psum", [128, 8 * 512], "float32"),
 }
-SEMAPHORES = (["ldst", "ldtg", "ldtab", "ldw", "rowm", "rowl", "styy", "iot", "ms", "qt", "qw", "ymm", "ycp", "lsem"]
+SEMAPHORES = (["ldst", "ldtg", "ldtab", "ldw", "rowm", "rowl", "styy", "iot", "ms", "qt", "qw", "ymm", "ycp", "lsem", "qin", "ua", "uu"]
               + ["idin%d" % j for j in range(N)] + ["ein%d" % j for j in range(N)]
-              + ["rc%d" % k for k in range(2)] + ["rs%d" % k for k in range(2)]
-              + ["%s%d" % (n, k) for n in ("ka", "ku", "kk") for k in range(3)]
+              + ["rc%d" % k for k in range(4)] + ["rs%d" % k for k in range(4)]
+              + ["%s%d" % (n, k) for n in ("ka", "ku", "kk") for k in (1, 2)]
+              + ["%s%d" % (n, k) for n in ("xa", "xk") for k in range(5)]
+              + ["%s%d" % (n, k) for n in ("xo", "xq") for k in range(4)]
               + ["%s%d" % (n, k) for n in ("bc", "oh", "qo", "cp", "qe") for k in range(N)]
               + ["mm%d%d" % (k, f) for k in range(N) for f in range(4)])
 
@@ -77,27 +85,16 @@ def make_plan(T, topo):
     C = list(T.cores)
     may = topo.may_write
     need = [[d for d in range(N) if d != j and not may(C[j], C[d])] for j in range(N)]
-    relay, relay_jobs, id_relay, id_partner = {}, {}, {}, {}
+    flows = []
     for j in range(N):
-        if not need[j]:
-            continue
-        xs = [x for x in range(128) if topo.chip(x) == topo.chip(C[j]) and topo.die(x) == topo.die(C[j]) and x not in C
-              and all(may(x, C[d]) for d in need[j])]
-        partner = [q for q in range(N) if q != j and topo.chip(C[q]) == topo.chip(C[j])
-                   and all(may(C[q], C[d]) for d in need[j])][0]
-        direct_back = [d for d in need[j] if may(C[d], C[j])]
-        both = [d for d in need[j] if d not in direct_back]
-        for part in (direct_back, both):
-            for k, d in enumerate(part):
-                x = xs[k % len(xs)]
-                jobs = relay_jobs.setdefault(x, [])
-                relay[j, d] = (x, len(jobs))
-                jobs.append((j, d))
-        for d in direct_back:
-            id_relay[j, d] = relay[j, d][0]
-        for d in both:
-            id_partner[j, d] = partner
-    late = [[j for j in range(N) if r in need[j]] for r in range(N)]
+        for d in need[j]:
+            if (j, topo.chip(C[d])) not in flows:
+                flows.append((j, topo.chip(C[d])))
+
+    def relay_core(j, d):
+        near = flows.index((j, topo.chip(C[d]))) % 2 == 0
+        return [x for x in range(128) if x not in C and topo.die(x) == topo.die(C[j]) and may(C[j], x) and may(x, C[d])
+                and (topo.chip(x) == topo.chip(C[j]) if near else topo.mates(topo.chip(x), topo.chip(C[d])))][0]
 
     def far(r, d):
         if d in need[r]:
@@ -105,31 +102,58 @@ def make_plan(T, topo):
         if topo.chip(C[d]) == topo.chip(C[r]):
             return 3
         return 2 if topo.same_plane(topo.chip(C[d]), topo.chip(C[r])) else 1
+    late = [[j for j in range(N) if r in need[j]] for r in range(N)]
     mid = [sorted([j for j in range(N) if j != r and j not in late[r]], key=lambda d: far(r, d)) for r in range(N)]
+    ready, turn = [], 0
+    for r in range(N):
+        ready.append(late[r][turn % len(late[r])])
+        turn += len(late[r]) - 1
+    passed = [[j for j in late[r] if j != ready[r]] for r in range(N)]
+    partner = {}
+    for r in range(N):
+        for j in passed[r]:
+            partner[j, r] = [q for q in range(N) if q != j and topo.chip(C[q]) == topo.chip(C[j]) and may(C[q], C[r])][0]
+    makes = []
+    for j in range(N):
+        rs = sorted([r for r in range(N) if ready[r] == j], key=lambda r: (may(C[r], C[j]), r))
+        makes.append([rs[i:i + 2] for i in range(0, len(rs), 2)])
+
+    relay, jobs = {}, {}
+
+    def add(kind, j, d):
+        x = relay_core(j, d)
+        relay[kind, j, d] = (x, len(jobs.setdefault(x, [])))
+        jobs[x].append((kind, j, d))
+    for j in range(N):
+        for pair in makes[j]:
+            for r in pair:
+                add("o", j, r)
+    blocks, groups = [], []
+    for r in range(N):
+        m, l, q = mid[r], passed[r], [ready[r]]
+        if need[r]:
+            b = m[:2] + q + l + m[2:]
+            groups.append([m[:2], q + l, m[2:]])
+        else:
+            b = m[:2] + l + m[2:] + q
+            groups.append([m[:2], l + m[2:], q])
+        own_last = sum(len(p) for p in makes[r]) > 1
+        blocks.append(b + [r] if own_last else [r] + b)
+        for d in b:
+            if d in need[r]:
+                add("e", r, d)
 
     idcalls = {}
     for j in range(N):
-        direct = [d for d in range(N) if d != j and may(C[j], C[d])]
-        calls = []
-        if not need[j]:
-            on = [C[d] for d in direct if topo.chip(C[d]) == topo.chip(C[j])]
-            off = [C[d] for d in direct if topo.chip(C[d]) != topo.chip(C[j])]
-            calls.append([(bits(topo.mask(C[j], on[0]))[-1], on), (bits(topo.mask(C[j], off[0]))[0], off)])
-        else:
-            first = [C[q] for q in sorted(set(id_partner[j, d] for d in need[j] if (j, d) in id_partner))]
-            first += sorted(set(id_relay[j, d] for d in need[j] if (j, d) in id_relay))
-            rest = [C[d] for d in direct if C[d] not in first]
-            calls.append([(bits(topo.mask(C[j], c))[-1 - k], [c]) for k, c in enumerate(first)])
-            if rest:
-                calls.append([(m, [c]) for m, c in zip(deal(topo, C[j], rest), rest)])
-        for call in calls:
-            idcalls.setdefault(C[j], []).append((j, call))
-    for (j, d), q in sorted(id_partner.items()):
-        if not [v for v in idcalls[C[q]] if v[0] == j]:
-            ds = [C[x] for x in range(N) if id_partner.get((j, x)) == q]
-            idcalls[C[q]].append((j, [(bits(topo.mask(C[q], c))[1 + k], [c]) for k, c in enumerate(ds)]))
-    for (j, d), x in sorted(id_relay.items()):
-        idcalls.setdefault(x, []).append((j, [(topo.mask(x, C[d]), [C[d]])]))
+        direct = [C[d] for d in range(N) if d != j and may(C[j], C[d])]
+        on = [c for c in direct if topo.chip(c) == topo.chip(C[j])]
+        off = [c for c in direct if topo.chip(c) != topo.chip(C[j])]
+        call = [(bits(topo.mask(C[j], on[0]))[-1], on)]
+        if off:
+            call.append((bits(topo.mask(C[j], off[0]))[0], off))
+        idcalls.setdefault(C[j], []).append((j, call))
+    for (j, r), q in sorted(partner.items()):
+        idcalls[C[q]].append((j, [(bits(topo.mask(C[q], C[r]))[1], [C[r]])]))
     idcount = {}
     for calls in idcalls.values():
         for j, call in calls:
@@ -137,25 +161,22 @@ def make_plan(T, topo):
                 for c in ds:
                     idcount[c, j] = idcount.get((c, j), 0) + count(m)
 
-    seq, rounds, ecount = [], [], {}
-    for r in range(N):
-        m, l = mid[r], late[r]
-        if need[r]:
-            seq.append(m[:2] + l + m[2:])
-            groups = [m[:2], l, m[2:]]
-        else:
-            seq.append(m + l)
-            groups = [m[:2], m[2:], l] if len(m) > 3 else [m[:2], m[2:] + l]
-        rr = []
-        for ds in groups:
-            hop = [relay[r, d][0] if (r, d) in relay else C[d] for d in ds]
-            rr.append(list(zip(ds, hop, deal(topo, C[r], hop))))
-        rounds.append(rr)
-        for rnd in rr:
-            for d, hop, mask in rnd:
-                ecount[r, d] = 2 * count(topo.mask(hop, C[d]) if (r, d) in relay else mask)
-    return dict(C=C, late=late, mid=mid, relay=relay, relay_jobs=relay_jobs, id_relay=id_relay, id_partner=id_partner,
-                idcalls=idcalls, idcount=idcount, seq=seq, rounds=rounds, ecount=ecount)
+    def rounds_of(kind, r, gs):
+        out = []
+        for ds in gs:
+            hop = [relay[kind, r, d][0] if (kind, r, d) in relay else C[d] for d in ds]
+            out.append(list(zip(ds, hop, deal(topo, C[r], hop))))
+        return out
+    rounds = {"o": [rounds_of("o", r, makes[r]) for r in range(N)], "e": [rounds_of("e", r, groups[r]) for r in range(N)]}
+    hopmask, lastcount = {}, {}
+    for kind in ("o", "e"):
+        for r in range(N):
+            for rnd in rounds[kind][r]:
+                for d, hop, mask in rnd:
+                    hopmask[kind, r, d] = mask
+                    lastcount[kind, r, d] = 2 * count(topo.mask(hop, C[d]) if (kind, r, d) in relay else mask)
+    return dict(C=C, mid=mid, passed=passed, ready=ready, makes=makes, relay=relay, jobs=jobs, partner=partner, blocks=blocks,
+                idcalls=idcalls, idcount=idcount, rounds=rounds, hopmask=hopmask, lastcount=lastcount)
 
 
 def dst_id(topo, c):
@@ -170,23 +191,26 @@ def send_ids(g, T, topo, j, call, own):
     return sum(count(m) for m, ds in call)
 
 
+def landing(T, kind, j, codes):
+    if kind == "o":
+        return (T.qcl if codes else T.qsl)[:], T.sem.qin
+    return (T.cl if codes else T.sl)[:, j * NC:(j + 1) * NC], T.sem["ein%d" % j]
+
+
 def relay_program(g, core, T, topo, P):
     sent = 0
-    for j, call in P["idcalls"].get(core, []):
-        g.wait_ge(T.sem["idin%d" % j], P["idcount"][core, j])
-        sent += send_ids(g, T, topo, j, call, False)
-    for k, (j, d) in enumerate(P["relay_jobs"][core]):
+    for k, (kind, j, d) in enumerate(P["jobs"][core]):
         c = P["C"][d]
-        m1 = [m for rnd in P["rounds"][j] for dd, hop, m in rnd if dd == d][0]
-        m2 = topo.mask(core, c)
+        m1, m2 = P["hopmask"][kind, j, d], topo.mask(core, c)
         rid, pid = topo.addr(c)[0], topo.addr(c)[1]
-        lo, hi = k * NC, (k + 1) * NC
-        g.wait_ge(T.sem["rc%d" % k], count(m1))
-        g.remote_dma(T.cl[:, j * NC:(j + 1) * NC].bitcast(dt.uint8), T.rc[:, lo:hi].bitcast(dt.uint8),
-                     T.sem["ein%d" % j], T.sem.lsem, pid, rid, m2)
-        g.wait_ge(T.sem["rs%d" % k], count(m1))
-        g.remote_dma(T.sl[:, j * NC:(j + 1) * NC], T.rs[:, lo:hi], T.sem["ein%d" % j], T.sem.lsem, pid, rid, m2)
-        sent += 2 * count(m2)
+        for codes in (True, False):
+            land, sem = landing(T, kind, j, codes)
+            src = (T.rc if codes else T.rs)[:, k * NC:(k + 1) * NC]
+            if codes:
+                src, land = src.bitcast(dt.uint8), land.bitcast(dt.uint8)
+            g.wait_ge(T.sem["%s%d" % ("rc" if codes else "rs", k)], count(m1))
+            g.remote_dma(land, src, sem, T.sem.lsem, pid, rid, m2)
+            sent += count(m2)
     g.wait_ge(T.sem.lsem, sent)
 
 
@@ -194,12 +218,13 @@ def rank_program(g, core, T, topo):
     P = make_plan(T, topo)
     me = T.rank_of(core)
     if me is None:
-        if core in P["relay_jobs"]:
+        if core in P["jobs"]:
             relay_program(g, core, T, topo, P)
         return
-    C, mid, late = P["C"], P["mid"][me], P["late"][me]
-    order = [me] + P["seq"][me]
-    kl = order.index(late[0])
+    C, mid, late, ready = P["C"], P["mid"][me], P["passed"][me], P["ready"][me]
+    order = P["blocks"][me]
+    makes = [r for pair in P["makes"][me] for r in pair]
+    k_own, k_ready = order.index(me), order.index(ready)
     nm = len(mid)
     S = T.sem
     V, A, PE, SY = g.vector, g.scalar, g.tensor, g.sync
@@ -209,30 +234,32 @@ def rank_program(g, core, T, topo):
     SY.dma_start(T.tgb[:], T.tg[:]).then_inc(S.ldtg, 16)
     SY.dma_start(T.tabb[:], T.tab[:]).then_inc(S.ldtab, 16)
     SY.dma_start(T.wb[:], T.w[:]).then_inc(S.ldw, 16)
-    SY.wait_ge(S.ms, 2)
+    SY.wait_ge(S.ms, 1)
     for ranks, buf, sem in ((mid, T.rm, S.rowm), (late, T.rl, S.rowl)):
         for i in reversed(range(len(ranks))):
             j = ranks[i]
             SY.wait_ge(S["idin%d" % j], P["idcount"][core, j])
             SY.dma_start(buf[32 * i:32 * i + 1, :], T.idin[j]).then_inc(sem, 16)
 
-    rows_m, rows_l = 32 * (nm - 1) + 1, 32 * (len(late) - 1) + 1
+    rows_m = 32 * (nm - 1) + 1
     V.memset(T.rm[0:rows_m, :], 0.0).then_inc(S.ms, 1)
-    V.memset(T.rl[0:rows_l, :], 0.0).then_inc(S.ms, 1)
 
     def keys(q, x, out, n):
-        a, t, u = [T.kt[0:n, (3 * q + i) * NC:(3 * q + i + 1) * NC] for i in range(3)]
-        V.tensor_scalar(a, x[0:n, 0:NC], float(me), 1024.0, OP.not_equal, OP.mult).then_inc(S["ka%d" % q], 1)
+        a, t, u = [T.kt[0:n, (3 * (q - 1) + i) * NC:(3 * (q - 1) + i + 1) * NC] for i in range(3)]
         V.tensor_scalar(t, x[0:n, NC:2 * NC], 4.0, -256.0, OP.mult, OP.add).then_inc(S["ka%d" % q], 1)
-        V.wait_ge(S["ka%d" % q], 2)
+        V.tensor_scalar(a, x[0:n, 0:NC], float(me), 1024.0, OP.not_equal, OP.mult).then_inc(S["ku%d" % q], 1)
+        V.wait_ge(S["ka%d" % q], 1)
         V.tensor_tensor(u, t, x[0:n, 2 * NC:3 * NC], OP.add).then_inc(S["ku%d" % q], 1)
-        V.wait_ge(S["ku%d" % q], 1)
+        V.wait_ge(S["ku%d" % q], 2)
         V.tensor_tensor(out, u, a, OP.add).then_inc(S["kk%d" % q], 1)
+
+    def compare(o, key, sem):
+        for b in range(4):
+            V.tensor_scalar(o[b], key, T.idx[:, b:b + 1], None, OP.is_equal).then_inc(sem, 1)
 
     def onehots(k):
         lo, hi = NC * k, NC * (k + 1)
-        for b in range(4):
-            V.tensor_scalar(T.o[:, 4 * lo + b:4 * hi:4], T.kb[:, lo:hi], T.idx[:, b:b + 1], None, OP.is_equal).then_inc(S["oh%d" % k], 1)
+        compare([T.o[:, 4 * lo + b:4 * hi:4] for b in range(4)], T.kb[:, lo:hi], S["oh%d" % k])
         V.wait_ge(S["oh%d" % k], 4)
         V.quantize_mx(T.co[:, lo:hi], T.so[:, lo:hi], T.o[:, 4 * lo:4 * hi]).then_inc(S["qo%d" % k], 1)
 
@@ -242,12 +269,17 @@ def rank_program(g, core, T, topo):
 
     def products(k):
         lo, hi = NC * k, NC * (k + 1)
-        PE.wait_ge(S["qo%d" % k], 1)
+        if k == k_ready:
+            PE.wait_ge(S.qin, P["lastcount"]["o", ready, me])
+            cx, sx = T.qcl[:], T.qsl[:]
+        else:
+            PE.wait_ge(S["qo%d" % k], 1)
+            cx, sx = T.co[:, lo:hi], T.so[:, lo:hi]
         if k >= 2:
             PE.wait_ge(S["cp%d" % (k - 2)], 4)
         for f in range(4):
-            PE.matmul_mx(bank(k, f), T.ct[:, NC * f:NC * (f + 1)], T.st[:, NC * f:NC * (f + 1)],
-                         T.co[:, lo:hi], T.so[:, lo:hi], True, True).then_inc(S["mm%d%d" % (k, f)], 1)
+            PE.matmul_mx(bank(k, f), T.ct[:, NC * f:NC * (f + 1)], T.st[:, NC * f:NC * (f + 1)], cx, sx, True, True
+                         ).then_inc(S["mm%d%d" % (k, f)], 1)
 
     def by_vector(k):
         return (0, 1) if k == N - 1 else ()
@@ -264,26 +296,58 @@ def rank_program(g, core, T, topo):
         V.quantize_mx(T.ce[:, lo:hi], T.se[:, lo:hi], T.e[:, 4 * lo:4 * hi]).then_inc(S["qe%d" % k], 1)
 
     V.wait_ge(S.ldtg, 16)
-    keys(0, T.tgb, T.kb[:, 0:NC], 128)
-    V.wait_ge(S.kk0, 1)
-    V.wait_ge(S.iot, 1)
-    onehots(0)
+    V.tensor_scalar(T.ko[:, 0:NC], T.tgb[:, NC:2 * NC], 4.0, -256.0, OP.mult, OP.add).then_inc(S.ua, 1)
+    todo = [[(makes.index(r), r) for r in pair] for pair in P["makes"][me]] + [[(4, me)]]
+    for n, part in enumerate(todo):
+        for i, r in part:
+            V.tensor_scalar(T.kx[:, NC * i:NC * (i + 1)], T.tgb[:, 0:NC], float(r), 1024.0, OP.not_equal, OP.mult).then_inc(S["xa%d" % i], 1)
+        if n == 0:
+            V.wait_ge(S.ua, 1)
+            V.tensor_tensor(T.ko[:, NC:2 * NC], T.ko[:, 0:NC], T.tgb[:, 2 * NC:3 * NC], OP.add).then_inc(S.uu, 1)
+            V.wait_ge(S.uu, 1)
+        for i, r in part:
+            out = T.kb[:, NC * k_own:NC * (k_own + 1)] if r == me else T.kq[:, NC * i:NC * (i + 1)]
+            V.wait_ge(S["xa%d" % i], 1)
+            V.tensor_tensor(out, T.ko[:, NC:2 * NC], T.kx[:, NC * i:NC * (i + 1)], OP.add).then_inc(S["xk%d" % i], 1)
+        if n == 0:
+            V.wait_ge(S.iot, 1)
+        for i, r in part:
+            if r != me:
+                V.wait_ge(S["xk%d" % i], 1)
+                compare([T.oq[:, 4 * NC * i + b:4 * NC * (i + 1):4] for b in range(4)], T.kq[:, NC * i:NC * (i + 1)], S["xo%d" % i])
+        for i, r in part:
+            if r != me:
+                V.wait_ge(S["xo%d" % i], 4)
+                V.quantize_mx(T.cq[:, NC * i:NC * (i + 1)], T.sq[:, NC * i:NC * (i + 1)], T.oq[:, 4 * NC * i:4 * NC * (i + 1)]
+                              ).then_inc(S["xq%d" % i], 1)
+    V.wait_ge(S.xk4, 1)
+    if k_own == 0:
+        onehots(0)
     V.wait_ge(S.ldtab, 16)
     V.quantize_mx(T.ct[:], T.st[:], T.tabb[:]).then_inc(S.qt, 1)
     V.wait_ge(S.ldw, 16)
     V.quantize_mx(T.cw[:], T.sw[:], T.wb[:]).then_inc(S.qw, 1)
-    entries(0)
+    if k_own == 0:
+        entries(0)
     V.wait_ge(S.rowm, 16 * nm)
     keys(1, T.rm, T.km[0:rows_m, :], rows_m)
-    for k in range(1, N):
-        if k == kl - 1:
-            V.wait_ge(S.rowl, 16 * len(late))
-            keys(2, T.rl, T.kl[0:rows_l, :], rows_l)
-        V.wait_ge(S["bc%d" % k], 1)
-        onehots(k)
-        if k > 1:
-            entries(k - 1)
-    entries(N - 1)
+    first = 1 if k_own == 0 else 0
+    spread = [k for k in range(N) if order[k] in mid or order[k] in late]
+    ahead = spread[max(spread.index(order.index(late[0])) - 2, 0)] if late else None
+    done = first
+    for k in range(first, N):
+        if k == ahead:
+            V.wait_ge(S.rowl, 16)
+            keys(2, T.rl, T.kl[0:1, :], 1)
+        if k in spread:
+            V.wait_ge(S["bc%d" % k], 1)
+        if k != k_ready:
+            onehots(k)
+            while done < k and (done != k_ready or done < k - 1):
+                entries(done)
+                done += 1
+    for k in range(done, N):
+        entries(k)
 
     for k in range(N):
         for f in range(4):
@@ -296,17 +360,17 @@ def rank_program(g, core, T, topo):
         products(k)
 
     def hops(r):
-        there = 2.5 if (me, r) in P["id_relay"] else 2 if (me, r) in P["id_partner"] else 1
-        back = 2 if (r, me) in P["relay"] else 1
+        there = 2 if (me, r) in P["partner"] or P["ready"][r] == me else 1
+        back = 2 if ("e", r, me) in P["relay"] else 1
         return there + back - (0.5 if topo.chip(C[r]) == topo.chip(core) else 0)
     others = sorted([r for r in range(N) if r != me], key=hops)
     PE.wait_ge(S["cp%d" % (N - 2)], 4)
-    PE.wait_ge(S.qe0, 1)
+    PE.wait_ge(S["qe%d" % k_own], 1)
     PE.wait_ge(S.qw, 1)
     ybank = bank(N - 2, 0)
-    PE.matmul_mx(ybank, T.cw[:], T.sw[:], T.ce[:, 0:NC], T.se[:, 0:NC], True, False)
+    PE.matmul_mx(ybank, T.cw[:], T.sw[:], T.ce[:, NC * k_own:NC * (k_own + 1)], T.se[:, NC * k_own:NC * (k_own + 1)], True, False)
     for i, r in enumerate(others):
-        PE.wait_ge(S["ein%d" % r], P["ecount"][r, me])
+        PE.wait_ge(S["ein%d" % r], P["lastcount"]["e", r, me])
         mm = PE.matmul_mx(ybank, T.cw[:], T.sw[:], T.cl[:, r * NC:(r + 1) * NC], T.sl[:, r * NC:(r + 1) * NC], False, i == N - 2)
     mm.then_inc(S.ymm, 1)
     A.wait_ge(S.ymm, 1)
@@ -323,29 +387,35 @@ def rank_program(g, core, T, topo):
             g.wait_ge(S["idin%d" % j], P["idcount"][core, j])
         sent += send_ids(g, T, topo, j, call, j == me)
 
-    for k in range(1, N):
+    def send_round(kind, rnd):
+        out = 0
+        for d, hop, m in rnd:
+            g.wait_ge(S["xq%d" % makes.index(d) if kind == "o" else "qe%d" % order.index(d)], 1)
+        for codes in (True, False):
+            ts = []
+            for d, hop, m in rnd:
+                k = makes.index(d) if kind == "o" else order.index(d)
+                buf = (T.cq if codes else T.sq) if kind == "o" else (T.ce if codes else T.se)
+                src = buf[:, NC * k:NC * (k + 1)]
+                if (kind, me, d) in P["relay"]:
+                    q = P["relay"][kind, me, d][1]
+                    land, sem = (T.rc if codes else T.rs)[:, NC * q:NC * (q + 1)], S["%s%d" % ("rc" if codes else "rs", q)]
+                else:
+                    land, sem = landing(T, kind, me, codes)
+                if codes:
+                    src, land = src.bitcast(dt.uint8), land.bitcast(dt.uint8)
+                ts.append(RemoteDMATransfer(dst_ids=[dst_id(topo, hop)], dma_engine_mask=m, remote_sem=sem, srcs=[src], dsts=[land]))
+                out += count(m)
+            g.remote_dma_fused(ts, local_sem=S.lsem)
+        return out
+
+    for rnd in P["rounds"]["o"][me]:
+        sent += send_round("o", rnd)
+    for k in spread:
         j = order[k]
         src, i, kk = (T.km, mid.index(j), S.kk1) if j in mid else (T.kl, late.index(j), S.kk2)
         g.wait_ge(kk, 1)
         g.partition_broadcast(T.kb[:, NC * k:NC * (k + 1)], src[32 * i:32 * i + 1, :], 128).then_inc(S["bc%d" % k], 1)
-
-    for rnd in P["rounds"][me]:
-        for d, hop, m in rnd:
-            g.wait_ge(S["qe%d" % order.index(d)], 1)
-        for c in (True, False):
-            ts = []
-            for d, hop, m in rnd:
-                k = order.index(d)
-                lo, hi = NC * k, NC * (k + 1)
-                if (me, d) in P["relay"]:
-                    q = P["relay"][me, d][1]
-                    land, sem = (T.rc if c else T.rs)[:, NC * q:NC * (q + 1)], S["%s%d" % ("rc" if c else "rs", q)]
-                else:
-                    land, sem = (T.cl if c else T.sl)[:, NC * me:NC * (me + 1)], S["ein%d" % me]
-                src = (T.ce if c else T.se)[:, lo:hi]
-                if c:
-                    src, land = src.bitcast(dt.uint8), land.bitcast(dt.uint8)
-                ts.append(RemoteDMATransfer(dst_ids=[dst_id(topo, hop)], dma_engine_mask=m, remote_sem=sem, srcs=[src], dsts=[land]))
-                sent += count(m)
-            g.remote_dma_fused(ts, local_sem=S.lsem)
+    for rnd in P["rounds"]["e"][me]:
+        sent += send_round("e", rnd)
     g.wait_ge(S.lsem, sent)

from concourse.bass import DstId, RemoteDMATransfer
from concourse.mybir import dt, AluOpType, ActivationFunctionType

N = 6
NC = 128
MX = "float8_e4m3fn_x4"

SCRATCH = {
    "idout": ("dram", [128, 3], "bfloat16"),
    "idin": ("dram", [N, 128, 3], "bfloat16"),
    "tgb": ("sbuf", [128, 3 * NC], "bfloat16"),
    "rm": ("sbuf", [128, 3 * NC], "bfloat16"),
    "rl": ("sbuf", [128, 3 * NC], "bfloat16"),
    "kt": ("sbuf", [128, 6 * NC], "bfloat16"),
    "km": ("sbuf", [128, NC], "bfloat16"),
    "kl": ("sbuf", [128, NC], "bfloat16"),
    "ko": ("sbuf", [128, 2 * NC], "bfloat16"),
    "kx": ("sbuf", [128, 5 * NC], "bfloat16"),
    "kb": ("sbuf", [128, N * NC], "bfloat16"),
    "kq": ("sbuf", [128, 4 * NC], "bfloat16"),
    "idx": ("sbuf", [128, 4], "bfloat16"),
    "tabb": ("sbuf", [128, 2048], "bfloat16"),
    "ct": ("sbuf", [128, 512], MX), "st": ("sbuf", [128, 512], "uint8"),
    "wb": ("sbuf", [128, 512], "bfloat16"),
    "cw": ("sbuf", [128, 128], MX), "sw": ("sbuf", [128, 128], "uint8"),
    "o": ("sbuf", [128, 4 * N * NC], "bfloat16"),
    "co": ("sbuf", [128, N * NC], MX), "so": ("sbuf", [128, N * NC], "uint8"),
    "oq": ("sbuf", [128, 4 * 4 * NC], "bfloat16"),
    "cq": ("sbuf", [128, 4 * NC], MX), "sq": ("sbuf", [128, 4 * NC], "uint8"),
    "qcl": ("sbuf", [128, NC], MX), "qsl": ("sbuf", [128, NC], "uint8"),
    "e": ("sbuf", [128, 4 * N * NC], "bfloat16"),
    "ce": ("sbuf", [128, N * NC], MX), "se": ("sbuf", [128, N * NC], "uint8"),
    "cl": ("sbuf", [128, N * NC], MX), "sl": ("sbuf", [128, N * NC], "uint8"),
    "rc": ("sbuf", [128, 4 * NC], MX), "rs": ("sbuf", [128, 4 * NC], "uint8"),
    "ysb": ("sbuf", [128, NC], "float32"),
    "z": ("psum", [128, 8 * 512], "float32"),
}
SEMAPHORES = (["ldst", "ldtg", "ldtab", "ldw", "rowm", "rowl", "styy", "iot", "ms", "qt", "qw", "ymm", "ycp", "lsem", "qin", "ua", "uu"]
              + ["idin%d" % j for j in range(N)] + ["ein%d" % j for j in range(N)]
              + ["rc%d" % k for k in range(4)] + ["rs%d" % k for k in range(4)]
              + ["%s%d" % (n, k) for n in ("ka", "ku", "kk") for k in (1, 2)]
              + ["%s%d" % (n, k) for n in ("xa", "xk") for k in range(5)]
              + ["%s%d" % (n, k) for n in ("xo", "xq") for k in range(4)]
              + ["%s%d" % (n, k) for n in ("bc", "oh", "qo", "cp", "qe") for k in range(N)]
              + ["mm%d%d" % (k, f) for k in range(N) for f in range(4)])


def bits(mask):
    return [1 << i for i in range(16) if (mask >> i) & 1]


def count(mask):
    return len(bits(mask))


def share(engines, k):
    size = 1
    while size * 2 * k <= len(engines):
        size *= 2
    extra, pos, out = (len(engines) - size * k) // size, 0, []
    for i in range(k):
        n = size * 2 if i < extra else size
        out.append(sum(engines[pos:pos + n]))
        pos += n
    return out


def deal(topo, src, dsts):
    off = [d for d in dsts if topo.chip(d) != topo.chip(src)]
    on = [d for d in dsts if topo.chip(d) == topo.chip(src)]
    got, free = {}, None
    if on:
        free = bits(topo.mask(src, on[0]))
    if off:
        eng = bits(topo.mask(src, off[0]))
        got.update(zip(off, share(eng, len(off))))
        if on:
            free = [b for b in free if b not in eng]
    if on:
        got.update(zip(on, share(free, len(on))))
    return [got[d] for d in dsts]


def make_plan(T, topo):
    C = list(T.cores)
    may = topo.may_write
    need = [[d for d in range(N) if d != j and not may(C[j], C[d])] for j in range(N)]
    flows = []
    for j in range(N):
        for d in need[j]:
            if (j, topo.chip(C[d])) not in flows:
                flows.append((j, topo.chip(C[d])))

    def relay_core(j, d):
        near = flows.index((j, topo.chip(C[d]))) % 2 == 0
        return [x for x in range(128) if x not in C and topo.die(x) == topo.die(C[j]) and may(C[j], x) and may(x, C[d])
                and (topo.chip(x) == topo.chip(C[j]) if near else topo.mates(topo.chip(x), topo.chip(C[d])))][0]

    def far(r, d):
        if d in need[r]:
            return 0
        if topo.chip(C[d]) == topo.chip(C[r]):
            return 3
        return 2 if topo.same_plane(topo.chip(C[d]), topo.chip(C[r])) else 1
    late = [[j for j in range(N) if r in need[j]] for r in range(N)]
    mid = [sorted([j for j in range(N) if j != r and j not in late[r]], key=lambda d: far(r, d)) for r in range(N)]
    ready, turn = [], 0
    for r in range(N):
        ready.append(late[r][turn % len(late[r])])
        turn += len(late[r]) - 1
    passed = [[j for j in late[r] if j != ready[r]] for r in range(N)]
    partner = {}
    for r in range(N):
        for j in passed[r]:
            partner[j, r] = [q for q in range(N) if q != j and topo.chip(C[q]) == topo.chip(C[j]) and may(C[q], C[r])][0]
    makes = []
    for j in range(N):
        rs = sorted([r for r in range(N) if ready[r] == j], key=lambda r: (may(C[r], C[j]), r))
        makes.append([rs[i:i + 2] for i in range(0, len(rs), 2)])

    relay, jobs = {}, {}

    def add(kind, j, d):
        x = relay_core(j, d)
        relay[kind, j, d] = (x, len(jobs.setdefault(x, [])))
        jobs[x].append((kind, j, d))
    for j in range(N):
        for pair in makes[j]:
            for r in pair:
                add("o", j, r)
    blocks, groups = [], []
    for r in range(N):
        m, l, q = mid[r], passed[r], [ready[r]]
        if need[r]:
            b = m[:2] + q + l + m[2:]
            groups.append([m[:2], q + l, m[2:]])
        else:
            b = m[:2] + l + m[2:] + q
            groups.append([m[:2], l + m[2:], q])
        own_last = sum(len(p) for p in makes[r]) > 1
        blocks.append(b + [r] if own_last else [r] + b)
        for d in b:
            if d in need[r]:
                add("e", r, d)

    idcalls = {}
    for j in range(N):
        direct = [C[d] for d in range(N) if d != j and may(C[j], C[d])]
        on = [c for c in direct if topo.chip(c) == topo.chip(C[j])]
        off = [c for c in direct if topo.chip(c) != topo.chip(C[j])]
        call = [(bits(topo.mask(C[j], on[0]))[-1], on)]
        if off:
            call.append((bits(topo.mask(C[j], off[0]))[0], off))
        idcalls.setdefault(C[j], []).append((j, call))
    for (j, r), q in sorted(partner.items()):
        idcalls[C[q]].append((j, [(bits(topo.mask(C[q], C[r]))[1], [C[r]])]))
    idcount = {}
    for calls in idcalls.values():
        for j, call in calls:
            for m, ds in call:
                for c in ds:
                    idcount[c, j] = idcount.get((c, j), 0) + count(m)

    def rounds_of(kind, r, gs):
        out = []
        for ds in gs:
            hop = [relay[kind, r, d][0] if (kind, r, d) in relay else C[d] for d in ds]
            out.append(list(zip(ds, hop, deal(topo, C[r], hop))))
        return out
    rounds = {"o": [rounds_of("o", r, makes[r]) for r in range(N)], "e": [rounds_of("e", r, groups[r]) for r in range(N)]}
    hopmask, lastcount = {}, {}
    for kind in ("o", "e"):
        for r in range(N):
            for rnd in rounds[kind][r]:
                for d, hop, mask in rnd:
                    hopmask[kind, r, d] = mask
                    lastcount[kind, r, d] = 2 * count(topo.mask(hop, C[d]) if (kind, r, d) in relay else mask)
    return dict(C=C, mid=mid, passed=passed, ready=ready, makes=makes, relay=relay, jobs=jobs, partner=partner, blocks=blocks,
                idcalls=idcalls, idcount=idcount, rounds=rounds, hopmask=hopmask, lastcount=lastcount)


def dst_id(topo, c):
    a = topo.addr(c)
    return DstId(rid=a[0], pnc=a[1])


def send_ids(g, T, topo, j, call, own):
    src = T.idout[:] if own else T.idin[j]
    g.remote_dma_fused([RemoteDMATransfer(dst_ids=[dst_id(topo, c) for c in ds], dma_engine_mask=m, remote_sem=T.sem["idin%d" % j],
                                          srcs=[src], dsts=[T.idin[j] for c in ds]) for m, ds in call], local_sem=T.sem.lsem)
    return sum(count(m) for m, ds in call)


def landing(T, kind, j, codes):
    if kind == "o":
        return (T.qcl if codes else T.qsl)[:], T.sem.qin
    return (T.cl if codes else T.sl)[:, j * NC:(j + 1) * NC], T.sem["ein%d" % j]


def relay_program(g, core, T, topo, P):
    sent = 0
    for k, (kind, j, d) in enumerate(P["jobs"][core]):
        c = P["C"][d]
        m1, m2 = P["hopmask"][kind, j, d], topo.mask(core, c)
        rid, pid = topo.addr(c)[0], topo.addr(c)[1]
        for codes in (True, False):
            land, sem = landing(T, kind, j, codes)
            src = (T.rc if codes else T.rs)[:, k * NC:(k + 1) * NC]
            if codes:
                src, land = src.bitcast(dt.uint8), land.bitcast(dt.uint8)
            g.wait_ge(T.sem["%s%d" % ("rc" if codes else "rs", k)], count(m1))
            g.remote_dma(land, src, sem, T.sem.lsem, pid, rid, m2)
            sent += count(m2)
    g.wait_ge(T.sem.lsem, sent)


def rank_program(g, core, T, topo):
    P = make_plan(T, topo)
    me = T.rank_of(core)
    if me is None:
        if core in P["jobs"]:
            relay_program(g, core, T, topo, P)
        return
    C, mid, late, ready = P["C"], P["mid"][me], P["passed"][me], P["ready"][me]
    order = P["blocks"][me]
    makes = [r for pair in P["makes"][me] for r in pair]
    k_own, k_ready = order.index(me), order.index(ready)
    nm = len(mid)
    S = T.sem
    V, A, PE, SY = g.vector, g.scalar, g.tensor, g.sync
    OP = AluOpType

    SY.dma_start(T.idout[:], T.tg[0:1, :]).then_inc(S.ldst, 16)
    SY.dma_start(T.tgb[:], T.tg[:]).then_inc(S.ldtg, 16)
    SY.dma_start(T.tabb[:], T.tab[:]).then_inc(S.ldtab, 16)
    SY.dma_start(T.wb[:], T.w[:]).then_inc(S.ldw, 16)
    SY.wait_ge(S.ms, 1)
    for ranks, buf, sem in ((mid, T.rm, S.rowm), (late, T.rl, S.rowl)):
        for i in reversed(range(len(ranks))):
            j = ranks[i]
            SY.wait_ge(S["idin%d" % j], P["idcount"][core, j])
            SY.dma_start(buf[32 * i:32 * i + 1, :], T.idin[j]).then_inc(sem, 16)

    rows_m = 32 * (nm - 1) + 1
    V.memset(T.rm[0:rows_m, :], 0.0).then_inc(S.ms, 1)

    def keys(q, x, out, n):
        a, t, u = [T.kt[0:n, (3 * (q - 1) + i) * NC:(3 * (q - 1) + i + 1) * NC] for i in range(3)]
        V.tensor_scalar(t, x[0:n, NC:2 * NC], 4.0, -256.0, OP.mult, OP.add).then_inc(S["ka%d" % q], 1)
        V.tensor_scalar(a, x[0:n, 0:NC], float(me), 1024.0, OP.not_equal, OP.mult).then_inc(S["ku%d" % q], 1)
        V.wait_ge(S["ka%d" % q], 1)
        V.tensor_tensor(u, t, x[0:n, 2 * NC:3 * NC], OP.add).then_inc(S["ku%d" % q], 1)
        V.wait_ge(S["ku%d" % q], 2)
        V.tensor_tensor(out, u, a, OP.add).then_inc(S["kk%d" % q], 1)

    def compare(o, key, sem):
        for b in range(4):
            V.tensor_scalar(o[b], key, T.idx[:, b:b + 1], None, OP.is_equal).then_inc(sem, 1)

    def onehots(k):
        lo, hi = NC * k, NC * (k + 1)
        compare([T.o[:, 4 * lo + b:4 * hi:4] for b in range(4)], T.kb[:, lo:hi], S["oh%d" % k])
        V.wait_ge(S["oh%d" % k], 4)
        V.quantize_mx(T.co[:, lo:hi], T.so[:, lo:hi], T.o[:, 4 * lo:4 * hi]).then_inc(S["qo%d" % k], 1)

    def bank(k, f):
        at = 512 * (4 * (k % 2) + f)
        return T.z[:, at:at + NC]

    def products(k):
        lo, hi = NC * k, NC * (k + 1)
        if k == k_ready:
            PE.wait_ge(S.qin, P["lastcount"]["o", ready, me])
            cx, sx = T.qcl[:], T.qsl[:]
        else:
            PE.wait_ge(S["qo%d" % k], 1)
            cx, sx = T.co[:, lo:hi], T.so[:, lo:hi]
        if k >= 2:
            PE.wait_ge(S["cp%d" % (k - 2)], 4)
        for f in range(4):
            PE.matmul_mx(bank(k, f), T.ct[:, NC * f:NC * (f + 1)], T.st[:, NC * f:NC * (f + 1)], cx, sx, True, True
                         ).then_inc(S["mm%d%d" % (k, f)], 1)

    def by_vector(k):
        return (0, 1) if k == N - 1 else ()

    def e_view(k, f):
        return T.e[:, 4 * NC * k + f:4 * NC * (k + 1):4]

    def entries(k):
        lo, hi = NC * k, NC * (k + 1)
        for f in by_vector(k):
            V.wait_ge(S["mm%d%d" % (k, f)], 1)
            V.tensor_copy(e_view(k, f), bank(k, f)).then_inc(S["cp%d" % k], 1)
        V.wait_ge(S["cp%d" % k], 4)
        V.quantize_mx(T.ce[:, lo:hi], T.se[:, lo:hi], T.e[:, 4 * lo:4 * hi]).then_inc(S["qe%d" % k], 1)

    V.wait_ge(S.ldtg, 16)
    V.tensor_scalar(T.ko[:, 0:NC], T.tgb[:, NC:2 * NC], 4.0, -256.0, OP.mult, OP.add).then_inc(S.ua, 1)
    todo = [[(makes.index(r), r) for r in pair] for pair in P["makes"][me]] + [[(4, me)]]
    for n, part in enumerate(todo):
        for i, r in part:
            V.tensor_scalar(T.kx[:, NC * i:NC * (i + 1)], T.tgb[:, 0:NC], float(r), 1024.0, OP.not_equal, OP.mult).then_inc(S["xa%d" % i], 1)
        if n == 0:
            V.wait_ge(S.ua, 1)
            V.tensor_tensor(T.ko[:, NC:2 * NC], T.ko[:, 0:NC], T.tgb[:, 2 * NC:3 * NC], OP.add).then_inc(S.uu, 1)
            V.wait_ge(S.uu, 1)
        for i, r in part:
            out = T.kb[:, NC * k_own:NC * (k_own + 1)] if r == me else T.kq[:, NC * i:NC * (i + 1)]
            V.wait_ge(S["xa%d" % i], 1)
            V.tensor_tensor(out, T.ko[:, NC:2 * NC], T.kx[:, NC * i:NC * (i + 1)], OP.add).then_inc(S["xk%d" % i], 1)
        if n == 0:
            V.wait_ge(S.iot, 1)
        for i, r in part:
            if r != me:
                V.wait_ge(S["xk%d" % i], 1)
                compare([T.oq[:, 4 * NC * i + b:4 * NC * (i + 1):4] for b in range(4)], T.kq[:, NC * i:NC * (i + 1)], S["xo%d" % i])
        for i, r in part:
            if r != me:
                V.wait_ge(S["xo%d" % i], 4)
                V.quantize_mx(T.cq[:, NC * i:NC * (i + 1)], T.sq[:, NC * i:NC * (i + 1)], T.oq[:, 4 * NC * i:4 * NC * (i + 1)]
                              ).then_inc(S["xq%d" % i], 1)
    V.wait_ge(S.xk4, 1)
    if k_own == 0:
        onehots(0)
    V.wait_ge(S.ldtab, 16)
    V.quantize_mx(T.ct[:], T.st[:], T.tabb[:]).then_inc(S.qt, 1)
    V.wait_ge(S.ldw, 16)
    V.quantize_mx(T.cw[:], T.sw[:], T.wb[:]).then_inc(S.qw, 1)
    if k_own == 0:
        entries(0)
    V.wait_ge(S.rowm, 16 * nm)
    keys(1, T.rm, T.km[0:rows_m, :], rows_m)
    first = 1 if k_own == 0 else 0
    spread = [k for k in range(N) if order[k] in mid or order[k] in late]
    ahead = spread[max(spread.index(order.index(late[0])) - 2, 0)] if late else None
    done = first
    for k in range(first, N):
        if k == ahead:
            V.wait_ge(S.rowl, 16)
            keys(2, T.rl, T.kl[0:1, :], 1)
        if k in spread:
            V.wait_ge(S["bc%d" % k], 1)
        if k != k_ready:
            onehots(k)
            while done < k and (done != k_ready or done < k - 1):
                entries(done)
                done += 1
    for k in range(done, N):
        entries(k)

    for k in range(N):
        for f in range(4):
            if f not in by_vector(k):
                A.wait_ge(S["mm%d%d" % (k, f)], 1)
                A.activation(e_view(k, f), bank(k, f), ActivationFunctionType.Copy).then_inc(S["cp%d" % k], 1)

    PE.wait_ge(S.qt, 1)
    for k in range(N):
        products(k)

    def hops(r):
        there = 2 if (me, r) in P["partner"] or P["ready"][r] == me else 1
        back = 2 if ("e", r, me) in P["relay"] else 1
        return there + back - (0.5 if topo.chip(C[r]) == topo.chip(core) else 0)
    others = sorted([r for r in range(N) if r != me], key=hops)
    PE.wait_ge(S["cp%d" % (N - 2)], 4)
    PE.wait_ge(S["qe%d" % k_own], 1)
    PE.wait_ge(S.qw, 1)
    ybank = bank(N - 2, 0)
    PE.matmul_mx(ybank, T.cw[:], T.sw[:], T.ce[:, NC * k_own:NC * (k_own + 1)], T.se[:, NC * k_own:NC * (k_own + 1)], True, False)
    for i, r in enumerate(others):
        PE.wait_ge(S["ein%d" % r], P["lastcount"]["e", r, me])
        mm = PE.matmul_mx(ybank, T.cw[:], T.sw[:], T.cl[:, r * NC:(r + 1) * NC], T.sl[:, r * NC:(r + 1) * NC], False, i == N - 2)
    mm.then_inc(S.ymm, 1)
    A.wait_ge(S.ymm, 1)
    A.activation(T.ysb[:], ybank, ActivationFunctionType.Copy).then_inc(S.ycp, 1)
    SY.wait_ge(S.ycp, 1)
    SY.dma_start(T.y[:], T.ysb[:]).then_inc(S.styy, 16)
    SY.wait_ge(S.styy, 16)

    sent = 0
    g.iota(T.idx[:], [[1, 4]], -256, 4, allow_small_or_imprecise_dtypes=True).then_inc(S.iot, 1)
    g.wait_ge(S.ldst, 16)
    for j, call in P["idcalls"][core]:
        if j != me:
            g.wait_ge(S["idin%d" % j], P["idcount"][core, j])
        sent += send_ids(g, T, topo, j, call, j == me)

    def send_round(kind, rnd):
        out = 0
        for d, hop, m in rnd:
            g.wait_ge(S["xq%d" % makes.index(d) if kind == "o" else "qe%d" % order.index(d)], 1)
        for codes in (True, False):
            ts = []
            for d, hop, m in rnd:
                k = makes.index(d) if kind == "o" else order.index(d)
                buf = (T.cq if codes else T.sq) if kind == "o" else (T.ce if codes else T.se)
                src = buf[:, NC * k:NC * (k + 1)]
                if (kind, me, d) in P["relay"]:
                    q = P["relay"][kind, me, d][1]
                    land, sem = (T.rc if codes else T.rs)[:, NC * q:NC * (q + 1)], S["%s%d" % ("rc" if codes else "rs", q)]
                else:
                    land, sem = landing(T, kind, me, codes)
                if codes:
                    src, land = src.bitcast(dt.uint8), land.bitcast(dt.uint8)
                ts.append(RemoteDMATransfer(dst_ids=[dst_id(topo, hop)], dma_engine_mask=m, remote_sem=sem, srcs=[src], dsts=[land]))
                out += count(m)
            g.remote_dma_fused(ts, local_sem=S.lsem)
        return out

    for rnd in P["rounds"]["o"][me]:
        sent += send_round("o", rnd)
    for k in spread:
        j = order[k]
        src, i, kk = (T.km, mid.index(j), S.kk1) if j in mid else (T.kl, late.index(j), S.kk2)
        g.wait_ge(kk, 1)
        g.partition_broadcast(T.kb[:, NC * k:NC * (k + 1)], src[32 * i:32 * i + 1, :], 128).then_inc(S["bc%d" % k], 1)
    for rnd in P["rounds"]["e"][me]:
        sent += send_round("e", rnd)
    g.wait_ge(S.lsem, sent)
